import numpy as np
import ml_dtypes


def mxq(x, axis, fmt="e4m3"):
    dtype, down = {"e4m3": (ml_dtypes.float8_e4m3fn, 7), "e5m2": (ml_dtypes.float8_e5m2, 14)}[fmt]
    v = np.moveaxis(np.asarray(x, np.float32).astype(ml_dtypes.bfloat16).astype(np.float64), axis, -1)
    blocks = v.reshape(v.shape[:-1] + (-1, 32))
    amax = np.abs(blocks).max(-1, keepdims=True)
    byte = np.maximum(np.where(amax > 0, np.frexp(amax)[1] - 1 + 127, 0) - down, 1)
    scale = np.exp2(byte - 127.0)
    codes = (blocks / scale).astype(np.float32).astype(dtype).astype(np.float64)
    return np.moveaxis((codes * scale).reshape(v.shape), -1, axis)


WIDE = False


def mx_kscale(k):
    if not WIDE:
        return np.ones(k)
    levels = np.array([10, -10, 5, -5, 0])
    if k % 512:
        return np.exp2(np.random.permutation(np.resize(levels, k // 32))).repeat(32)
    a = np.empty((k // 512, 16))
    for p in range(k // 512):
        a[p, :8] = np.random.permutation(np.resize(levels, 8))
        for g in range(8):
            far = levels[np.abs(levels - a[p, g]) >= 10]
            a[p, g + 8] = far[np.random.randint(len(far))]
    return np.exp2(a.ravel()).repeat(32)


def f64(x):
    return np.asarray(x).astype(np.float64)


def striped(idx):
    return np.tile(idx.reshape(-1, 16).T, (8, 1)).astype(np.uint16)


def unstriped(offs):
    return offs[:16].T.reshape(-1).astype(np.int64)


def striped8(idx):
    return np.concatenate([x.reshape(-1, 16).T for x in idx]).astype(np.uint16)


def runs(offs, k):
    lists = np.stack([offs[16 * r : 16 * r + 16].T.reshape(-1) for r in range(8)]).astype(np.int64)
    return lists[np.arange(k) % 512 // 64]


def pack_weight(w):
    k, n = w.shape
    w = f64(np.asarray(w, np.float32).astype(ml_dtypes.bfloat16)).reshape(k // 32, 32, n)
    amax = np.abs(w).max(1)
    byte = np.clip(np.where(amax > 0, np.frexp(amax)[1] - 1 + 127 - 7, 1), 1, 254)
    scaled = (w * np.exp2(127.0 - byte)[:, None, :]).reshape(k, n).astype(np.float32)
    words = np.ascontiguousarray(scaled.reshape(k // 512, 128, 4, n).transpose(0, 1, 3, 2)).astype(ml_dtypes.float8_e4m3fn).view(np.uint8)
    return words, np.ascontiguousarray(byte.astype(np.uint8).reshape(k // 512, 16, n))


def unpack_weight(words, scales):
    g, p, n, _ = words.shape
    vals = np.ascontiguousarray(words).view(ml_dtypes.float8_e4m3fn).astype(np.float64) * np.repeat(np.exp2(scales.astype(np.float64) - 127.0), 8, axis=1)[..., None]
    return vals.transpose(0, 1, 3, 2).reshape(g * 512, n)


def sigmoid(v):
    return 1.0 / (1.0 + np.exp(-np.maximum(v, -700.0)))

def planes(y):
    n, m = y.shape
    v = y.astype(np.float32).astype(ml_dtypes.bfloat16).astype(np.float64).reshape(n // 32, 32, m)
    top = np.abs(v).max(1)
    byte = np.clip(np.where(top > 0, np.frexp(top)[1] - 1 + 127 - 7, 1), 1, 254)
    codes = (v * np.exp2(127.0 - byte)[:, None, :]).reshape(n, m).astype(np.float32).astype(ml_dtypes.float8_e4m3fn).view(np.uint8)
    words = codes.reshape(n // 512, 128, 4, m).transpose(0, 1, 3, 2)
    return np.ascontiguousarray(words), np.ascontiguousarray(byte.astype(np.uint8).reshape(n // 512, 16, m))


K, T, S, N, H, G, W = 512, 1024, 256, 512, 512, 2048, 128


def setup_inputs():
    n = np.random.standard_normal
    s = mx_kscale(K)[:, None]
    u = mx_kscale(K)
    packed_xT = pack_weight(n((K, T)) * s)
    packed_w1 = pack_weight(n((K, H)) / np.sqrt(K) / s)
    packed_dT = pack_weight(n((K, G)) / s)
    packed_w2 = pack_weight(n((H, N)) / np.sqrt(2 * H) / u[:, None])
    packed_w3 = pack_weight(n((H, N)) / np.sqrt(2 * H) / u[:, None])
    perm = np.random.permutation(S)
    return {
        "x_words": packed_xT[0],
        "x_scales": packed_xT[1],
        "w1_words": packed_w1[0],
        "w1_scales": packed_w1[1],
        "d_words": packed_dT[0],
        "d_scales": packed_dT[1],
        "gn": (np.random.uniform(0.5, 1.5, (H, 1)) * u[:, None]).astype(np.float32),
        "gk": (np.random.uniform(0.5, 1.5, (H, 1)) * u[:, None]).astype(np.float32),
        "w2_words": packed_w2[0],
        "w2_scales": packed_w2[1],
        "w3_words": packed_w3[0],
        "w3_scales": packed_w3[1],
        "offs": striped(np.random.permutation(T)[:S]),
        "kidx": striped8(np.random.randint(0, G, (8, H))),
        "two": striped(np.random.permutation(T)[:S]),
        "n1": striped(np.random.permutation(S)),
        "n2": striped(np.random.permutation(S)),
        "n3": striped(np.random.permutation(S)),
        "n4": striped8(np.stack([np.random.permutation(S) for _ in range(8)])),
        "n5": striped8(np.stack([np.random.permutation(S) for _ in range(8)])),
        "n6": striped(perm[:W]),
        "n7": striped(perm[W:]),
    }


def reference(x_words, x_scales, w1_words, w1_scales, d_words, d_scales, gn, gk, w2_words, w2_scales, w3_words, w3_scales, offs, kidx, two, n1, n2, n3, n4, n5, n6, n7):
    xq = unpack_weight(x_words, x_scales)[:, unstriped(offs)]
    y = unpack_weight(w1_words, w1_scales).T @ xq
    z = f64(gn) * (y[:, unstriped(n1)] * sigmoid(y) + y[:, unstriped(n2)] * (sigmoid(y[:, unstriped(n3)])))
    d_kidx = unpack_weight(d_words, d_scales)[np.arange(K)[:, None], runs(kidx, K)]
    x_two = unpack_weight(x_words, x_scales)[:, unstriped(two)]
    s = 0.0625 * (d_kidx.T @ x_two)
    z2 = f64(gk) * (s[np.arange(H)[:, None], runs(n4, H)] + 0.75 * (s[np.arange(H)[:, None], runs(n5, H)]))
    h = unpack_weight(w2_words, w2_scales).T @ mxq(z, 0, "e4m3") + unpack_weight(w3_words, w3_scales).T @ mxq(z2, 0, "e4m3")
    pa = h[:, unstriped(n6)]
    pb = h[:, unstriped(n7)]
    ra = pa * sigmoid(pb)
    out = h.copy()
    out[:, unstriped(n7)] = ra
    return (out,) + planes(out)

@@ -1,0 +1,237 @@
+from contextlib import ExitStack
+
+import concourse.mybir as mybir
+
+F32 = mybir.dt.float32
+BF16 = mybir.dt.bfloat16
+I32 = mybir.dt.int32
+U32 = mybir.dt.uint32
+U16 = mybir.dt.uint16
+U8 = mybir.dt.uint8
+FP8X4 = mybir.dt.float8_e4m3fn_x4
+ALU = mybir.AluOpType
+ACT = mybir.ActivationFunctionType
+
+P = 128
+PACK = 4
+K, T, S, N, H, G, W = 512, 1024, 256, 512, 512, 2048, 128
+ONE_LIST_WINDOW = S + 16
+EIGHT_LIST_WINDOW = 2 * S
+
+FLOPS = 4 * 2 * K * H * S
+
+
+def tile_picked_jkeywsumsumfold_none_po_kernel(
+    tc, x_words, x_scales, w1_words, w1_scales, d_words, d_scales, gn, gk,
+    w2_words, w2_scales, w3_words, w3_scales,
+    offs, kidx, two, n1, n2, n3, n4, n5, n6, n7, out_0, out_1, out_2,
+):
+    nc = tc.nc
+    with ExitStack() as ctx:
+        sb = ctx.enter_context(tc.tile_pool(name="sb", bufs=1))
+        psum = ctx.enter_context(tc.psum_pool(name="psum", bufs=1))
+
+        def tile(name, shape, dtype, tag=None):
+            return sb.tile(shape, dtype, name=name, tag=tag or name, align_bytes=64)
+
+        def load_list(name, src):
+            lst = tile(name, list(src.shape), U16)
+            nc.sync.dma_start(lst[:], src)
+            return lst
+
+        def load_words(name, src, tag=None):
+            words = tile(name, [P, src.shape[2]], U32, tag)
+            nc.sync.dma_start(words[:].bitcast(I32), src[0].rearrange("p n t -> p (n t)").bitcast(I32))
+            return words
+
+        def zeroed_bytes(name, width, engine, tag=None):
+            plane = tile(name, [P, width], U8, tag)
+            engine.memset(plane[:].bitcast(I32), 0)
+            return plane
+
+        def load_scale_plane(name, src, quadrants, plane=None):
+            width = src.shape[2]
+            plane = tile(name, [P, width], U8) if plane is None else plane
+            for q in quadrants:
+                rows = src[0, 4 * q : 4 * q + 4, :].bitcast(I32)
+                nc.sync.dma_start(
+                    plane[32 * q : 32 * q + 32, :].bitcast(I32),
+                    rows.unsqueeze(0).to_broadcast([8, 4, width // 4]),
+                )
+            return plane
+
+        def load_scale_rows(plane, src, first, quadrants):
+            for q in quadrants:
+                nc.sync.dma_start(
+                    plane[32 * q + first : 32 * q + first + 4, :].bitcast(I32),
+                    src[0, 4 * q : 4 * q + 4, :].bitcast(I32),
+                )
+
+        def deal(copy, name, src, dtype, tag=None):
+            dealt = tile(name, [P, src.shape[1]], dtype, tag)
+            copy(
+                out=dealt[:].rearrange("p (t m) -> p m t", t=PACK),
+                in_=src[:].rearrange("p (m t) -> p m t", t=PACK),
+            )
+            return dealt
+
+        def gather(name, window, lst, dtype):
+            picked = tile(name, [P, lst.shape[1] * 16], dtype)
+            nc.vector.tensor_copy(out=picked[:], in_=window[:].indirect(lst[:]))
+            return picked
+
+        def mx(out, words, scales, t, rhs, rhs_scales, start, stop):
+            cols = slice(P * t, P * (t + 1))
+            nc.tensor.matmul_mx(
+                out=out, lhsT=words[:, cols].bitcast(FP8X4), lhsT_scale=scales[:, cols],
+                rhs=rhs[:].bitcast(FP8X4), rhs_scale=rhs_scales[:], start=start, stop=stop,
+            )
+
+        def quantise(name, grouped):
+            codes = tile(name + "_codes", [P, S], U32)
+            scales = tile(name + "_scales", [P, S], U8)
+            nc.vector.quantize_mx(out=codes[:].bitcast(FP8X4), scales=scales[:], in_=grouped[:])
+            return codes, scales
+
+        def add_and_group(name, a, b):
+            grouped = tile(name, [P, S * PACK], BF16)
+            nc.vector.tensor_tensor(
+                out=grouped[:].rearrange("p (c i t) -> p c t i", i=4, t=PACK),
+                in0=a[:].rearrange("p t (c i) -> p c t i", i=4),
+                in1=b[:].rearrange("p t (c i) -> p c t i", i=4),
+                op=ALU.add,
+            )
+            return grouped
+
+        def windows(name, width, engine):
+            tiles = [tile("%s%d" % (name, t), [P, width], F32) for t in range(PACK)]
+            for win in tiles:
+                engine.memset(win[:, S:], 0.0)
+            return tiles
+
+        w1_plane = zeroed_bytes("w1_plane", H, nc.vector)
+        d_rows = zeroed_bytes("d_rows", G, nc.gpsimd)
+        key_plane = zeroed_bytes("key_plane", H, nc.vector)
+        sig_win = windows("sig_win", ONE_LIST_WINDOW, nc.vector)
+        y_win = windows("y_win", ONE_LIST_WINDOW, nc.vector)
+        s_win = windows("s_win", EIGHT_LIST_WINDOW, nc.vector)
+
+        offs_l = load_list("offs_l", offs)
+        x_plane = load_scale_plane("x_plane", x_scales, range(4))
+        load_scale_rows(w1_plane, w1_scales, 0, range(1))
+        x_tab = load_words("x_tab", x_words)
+        w1_raw = load_words("w1_raw", w1_words)
+        load_scale_rows(w1_plane, w1_scales, 0, range(1, 4))
+        kidx_l = load_list("kidx_l", kidx)
+        nc.sync.dma_start(d_rows[0:P:8, :].bitcast(I32), d_scales[0].bitcast(I32))
+        d_tab = load_words("d_tab", d_words)
+        two_l = load_list("two_l", two)
+        n3_l = load_list("n3_l", n3)
+        gn_t = tile("gn_t", [P, PACK], F32)
+        nc.sync.dma_start(gn_t[:], gn.rearrange("(p t) o -> p (t o)", t=PACK))
+        n1_l = load_list("n1_l", n1)
+        gk_t = tile("gk_t", [P, PACK], F32)
+        nc.sync.dma_start(gk_t[:], gk.rearrange("(p t) o -> p (t o)", t=PACK))
+        n4_l = load_list("n4_l", n4)
+        n5_l = load_list("n5_l", n5)
+        n2_l = load_list("n2_l", n2)
+        n7_l = load_list("n7_l", n7)
+        n6_l = load_list("n6_l", n6)
+
+        xq_s = gather("xq_s", x_plane, offs_l, U8)
+        xq_c = gather("xq_c", x_tab, offs_l, U32)
+        w1_c = deal(nc.vector.tensor_copy, "w1_c", w1_raw, U32)
+        w1_s = deal(nc.vector.tensor_copy, "w1_s", w1_plane, U8)
+        y_ps = [psum.tile([P, S], F32, name="y_ps%d" % t, tag="yh%d" % t) for t in range(PACK)]
+        for t in range(PACK):
+            mx(y_ps[t][:], w1_c, w1_s, t, xq_c, xq_s, True, True)
+        for t in range(PACK):
+            nc.scalar.activation(out=sig_win[t][:, :S], in_=y_ps[t][:], func=ACT.Sigmoid)
+
+        key_rows = gather("key_rows", d_rows, kidx_l, U8)
+        key_dealt = deal(nc.vector.tensor_copy, "key_dealt", key_rows, U8)
+        for q in range(4):
+            nc.sync.dma_start(
+                key_plane[32 * q : 32 * q + 4, :].bitcast(I32),
+                key_dealt[32 * q : 32 * q + 32 : 8, :].bitcast(I32),
+            )
+        xt_s = gather("xt_s", x_plane, two_l, U8)
+        xt_c = gather("xt_c", x_tab, two_l, U32)
+        w23_plane = zeroed_bytes("w23_plane", N, nc.vector, "x_plane")
+        load_scale_rows(w23_plane, w2_scales, 0, range(4))
+        load_scale_rows(w23_plane, w3_scales, 4, range(4))
+        w2_raw = load_words("w2_raw", w2_words, "x_tab")
+        w3_raw = load_words("w3_raw", w3_words, "key_rows")
+
+        sig3 = tile("sig3", [P, PACK, S], F32)
+        y1 = tile("y1", [P, PACK, S], F32)
+        for t in range(PACK):
+            nc.scalar.activation(out=sig3[:, t, :], in_=sig_win[t][:].indirect(n3_l[:]), func=ACT.Copy)
+        for t in range(PACK):
+            nc.vector.tensor_scalar(
+                out=y_win[t][:, :S], in0=y_ps[t][:], scalar1=gn_t[:, t : t + 1], scalar2=None, op0=ALU.mult
+            )
+        for t in range(PACK):
+            nc.scalar.activation(out=y1[:, t, :], in_=y_win[t][:].indirect(n1_l[:]), func=ACT.Copy)
+
+        key_words = gather("key_words", d_tab, kidx_l, U32)
+        key_c = deal(nc.vector.tensor_copy, "key_c", key_words, U32)
+        s_ps = [psum.tile([P, S], F32, name="s_ps%d" % t) for t in range(PACK)]
+        for t in range(PACK):
+            mx(s_ps[t][:], key_c, key_plane, t, xt_c, xt_s, True, True)
+        for t in range(PACK):
+            nc.scalar.activation(out=s_win[t][:, :S], in_=s_ps[t][:], func=ACT.Copy, scale=gk_t[:, t : t + 1])
+        s4 = tile("s4", [P, PACK, S], F32)
+        s5 = tile("s5", [P, PACK, S], F32)
+        for t in range(PACK):
+            nc.scalar.activation(out=s4[:, t, :], in_=s_win[t][:].indirect(n4_l[:]), func=ACT.Copy, scale=0.0625)
+            nc.scalar.activation(out=s5[:, t, :], in_=s_win[t][:].indirect(n5_l[:]), func=ACT.Copy, scale=0.75 * 0.0625)
+
+        w3_c = deal(nc.scalar.copy, "w3_c", w3_raw, U32, "s_win3")
+        za = tile("za", [P, PACK, S], F32)
+        zb = tile("zb", [P, PACK, S], F32)
+        for t in range(PACK):
+            nc.vector.tensor_tensor(
+                out=za[:, t, :], in0=y_win[t][:].indirect(n2_l[:]), in1=sig3[:, t, :], op=ALU.mult
+            )
+        for t in range(PACK):
+            nc.vector.tensor_tensor(out=zb[:, t, :], in0=y1[:, t, :], in1=sig_win[t][:, :S], op=ALU.mult)
+        z_c, z_s = quantise("z", add_and_group("z_grouped", za, zb))
+        w2_c = deal(nc.vector.tensor_copy, "w2_c", w2_raw, U32)
+        w23_s = deal(nc.vector.tensor_copy, "w23_s", w23_plane, U8)
+        h_ps = [psum.tile([P, S], F32, name="h_ps%d" % t, tag="yh%d" % t) for t in range(PACK)]
+        for t in range(PACK):
+            mx(h_ps[t][:], w2_c, w23_s, t, z_c, z_s, True, False)
+
+        z2_c, z2_s = quantise("z2", add_and_group("z2_grouped", s4, s5))
+        for t in range(PACK):
+            mx(h_ps[t][:], w3_c, w23_s[4:P, :], t, z2_c, z2_s, False, True)
+
+        out_rows = out_0.rearrange("(p t) s -> p t s", t=PACK)
+        out_grouped = tile("out_grouped", [P, S, PACK], BF16)
+        h_win = [tile("h_win%d" % t, [P, S], F32) for t in range(PACK)]
+        gate = [tile("gate%d" % t, [P, W], F32) for t in range(PACK)]
+        ra = [tile("ra%d" % t, [P, W], F32) for t in range(PACK)]
+        for t in range(PACK):
+            nc.vector.tensor_copy(out=h_win[t][:], in_=h_ps[t][:])
+        for t in range(PACK):
+            nc.scalar.activation(out=gate[t][:], in_=h_win[t][:].indirect(n7_l[:]), func=ACT.Sigmoid)
+            nc.vector.tensor_tensor(
+                out=ra[t][:], in0=h_win[t][:].indirect(n6_l[:]), in1=gate[t][:], op=ALU.mult
+            )
+        for t in range(PACK):
+            nc.scalar.activation(out=h_win[t][:].indirect(n7_l[:]), in_=ra[t][:], func=ACT.Copy)
+            nc.sync.dma_start(out_rows[:, t, :], h_win[t][:])
+            nc.vector.tensor_copy(out=out_grouped[:, :, t], in_=h_win[t][:])
+
+        out_c = tile("out_c", [P, S], U32)
+        out_s = tile("out_s", [P, S], U8)
+        nc.vector.quantize_mx(
+            out=out_c[:].bitcast(FP8X4), scales=out_s[:], in_=out_grouped[:].rearrange("p s t -> p (s t)")
+        )
+        nc.sync.dma_start(out_1[0].rearrange("p n t -> p (n t)").bitcast(I32), out_c[:].bitcast(I32))
+        for q in range(4):
+            eng = nc.scalar if q % 2 else nc.sync
+            eng.dma_start(
+                out_2[0, 4 * q : 4 * q + 4, :].bitcast(I32), out_s[32 * q : 32 * q + 4, :].bitcast(I32)
+            )

@@ -84,21 +84,22 @@ def tile_picked_jkeywsumsumfold_none_po_kernel(
             cols = slice(P * t, P * (t + 1))
             nc.tensor.matmul_mx(
                 out=out, lhsT=words[:, cols].bitcast(FP8X4), lhsT_scale=scales[:, cols],
-                rhs=rhs[:].bitcast(FP8X4), rhs_scale=rhs_scales[:], start=start, stop=stop,
+                rhs=rhs.bitcast(FP8X4), rhs_scale=rhs_scales, start=start, stop=stop,
             )
 
         def quantise(name, grouped):
-            codes = tile(name + "_codes", [P, S], U32)
-            scales = tile(name + "_scales", [P, S], U8)
+            width = grouped.shape[1] // PACK
+            codes = tile(name + "_codes", [P, width], U32)
+            scales = tile(name + "_scales", [P, width], U8)
             nc.vector.quantize_mx(out=codes[:].bitcast(FP8X4), scales=scales[:], in_=grouped[:])
             return codes, scales
 
-        def add_and_group(name, a, b):
-            grouped = tile(name, [P, S * PACK], BF16)
+        def add_and_group(name, a, b, tag=None):
+            grouped = tile(name, [P, a.shape[2] * PACK], BF16, tag)
             nc.vector.tensor_tensor(
                 out=grouped[:].rearrange("p (c i t) -> p c t i", i=4, t=PACK),
-                in0=a[:].rearrange("p t (c i) -> p c t i", i=4),
-                in1=b[:].rearrange("p t (c i) -> p c t i", i=4),
+                in0=a.rearrange("p t (c i) -> p c t i", i=4),
+                in1=b.rearrange("p t (c i) -> p c t i", i=4),
                 op=ALU.add,
             )
             return grouped
@@ -124,12 +125,12 @@ def tile_picked_jkeywsumsumfold_none_po_kernel(
         load_scale_rows(w1_plane, w1_scales, 0, range(1, 4))
         kidx_l = load_list("kidx_l", kidx)
         nc.sync.dma_start(d_rows[0:P:8, :].bitcast(I32), d_scales[0].bitcast(I32))
-        d_tab = load_words("d_tab", d_words)
-        two_l = load_list("two_l", two)
-        n3_l = load_list("n3_l", n3)
         gn_t = tile("gn_t", [P, PACK], F32)
         nc.sync.dma_start(gn_t[:], gn.rearrange("(p t) o -> p (t o)", t=PACK))
         n1_l = load_list("n1_l", n1)
+        two_l = load_list("two_l", two)
+        d_tab = load_words("d_tab", d_words)
+        n3_l = load_list("n3_l", n3)
         gk_t = tile("gk_t", [P, PACK], F32)
         nc.sync.dma_start(gk_t[:], gk.rearrange("(p t) o -> p (t o)", t=PACK))
         n4_l = load_list("n4_l", n4)
@@ -141,10 +142,12 @@ def tile_picked_jkeywsumsumfold_none_po_kernel(
         xq_s = gather("xq_s", x_plane, offs_l, U8)
         xq_c = gather("xq_c", x_tab, offs_l, U32)
         w1_c = deal(nc.vector.tensor_copy, "w1_c", w1_raw, U32)
-        w1_s = deal(nc.vector.tensor_copy, "w1_s", w1_plane, U8)
+        w1_s = tile("w1_s", [P, H], U8)
+        for t in range(PACK):
+            nc.vector.tensor_copy(out=w1_s[:, P * t : P * (t + 1)], in_=w1_plane[:, t:H:PACK])
         y_ps = [psum.tile([P, S], F32, name="y_ps%d" % t, tag="yh%d" % t) for t in range(PACK)]
         for t in range(PACK):
-            mx(y_ps[t][:], w1_c, w1_s, t, xq_c, xq_s, True, True)
+            mx(y_ps[t][:], w1_c, w1_s, t, xq_c[:], xq_s[:], True, True)
         for t in range(PACK):
             nc.scalar.activation(out=sig_win[t][:, :S], in_=y_ps[t][:], func=ACT.Sigmoid)
 
@@ -155,65 +158,81 @@ def tile_picked_jkeywsumsumfold_none_po_kernel(
                 key_plane[32 * q : 32 * q + 4, :].bitcast(I32),
                 key_dealt[32 * q : 32 * q + 32 : 8, :].bitcast(I32),
             )
+        sig3 = tile("sig3", [P, PACK, S], F32)
+        y1 = tile("y1", [P, PACK, S], F32)
+        for t in range(PACK):
+            nc.vector.tensor_scalar(
+                out=y_win[t][:, :S], in0=y_ps[t][:], scalar1=gn_t[:, t : t + 1], scalar2=None, op0=ALU.mult
+            )
+        zb = tile("zb", [P, PACK, S], F32)
+        for t in range(PACK):
+            nc.scalar.activation(out=y1[:, t, :], in_=y_win[t][:].indirect(n1_l[:]), func=ACT.Copy)
+            nc.gpsimd.tensor_tensor(out=zb[:, t, :], in0=y1[:, t, :], in1=sig_win[t][:, :S], op=ALU.mult)
+        for t in range(PACK):
+            nc.scalar.activation(out=sig3[:, t, :], in_=sig_win[t][:].indirect(n3_l[:]), func=ACT.Copy)
         xt_s = gather("xt_s", x_plane, two_l, U8)
         xt_c = gather("xt_c", x_tab, two_l, U32)
         w23_plane = zeroed_bytes("w23_plane", N, nc.vector, "x_plane")
         load_scale_rows(w23_plane, w2_scales, 0, range(4))
         load_scale_rows(w23_plane, w3_scales, 4, range(4))
-        w2_raw = load_words("w2_raw", w2_words, "x_tab")
-        w3_raw = load_words("w3_raw", w3_words, "key_rows")
-
-        sig3 = tile("sig3", [P, PACK, S], F32)
-        y1 = tile("y1", [P, PACK, S], F32)
-        for t in range(PACK):
-            nc.scalar.activation(out=sig3[:, t, :], in_=sig_win[t][:].indirect(n3_l[:]), func=ACT.Copy)
-        for t in range(PACK):
-            nc.vector.tensor_scalar(
-                out=y_win[t][:, :S], in0=y_ps[t][:], scalar1=gn_t[:, t : t + 1], scalar2=None, op0=ALU.mult
-            )
-        for t in range(PACK):
-            nc.scalar.activation(out=y1[:, t, :], in_=y_win[t][:].indirect(n1_l[:]), func=ACT.Copy)
+        w23_raw = tile("w23_raw", [P, 2, N], U32, "x_tab")
+        for i, src in enumerate((w2_words, w3_words)):
+            nc.sync.dma_start(w23_raw[:, i, :].bitcast(I32), src[0].rearrange("p n t -> p (n t)").bitcast(I32))
 
         key_words = gather("key_words", d_tab, kidx_l, U32)
         key_c = deal(nc.vector.tensor_copy, "key_c", key_words, U32)
-        s_ps = [psum.tile([P, S], F32, name="s_ps%d" % t) for t in range(PACK)]
+        s_ps = [psum.tile([P, S], F32, name="s_ps%d" % t, tag="sh%d" % t) for t in range(PACK)]
         for t in range(PACK):
-            mx(s_ps[t][:], key_c, key_plane, t, xt_c, xt_s, True, True)
+            mx(s_ps[t][:], key_c, key_plane, t, xt_c[:], xt_s[:], True, True)
         for t in range(PACK):
             nc.scalar.activation(out=s_win[t][:, :S], in_=s_ps[t][:], func=ACT.Copy, scale=gk_t[:, t : t + 1])
         s4 = tile("s4", [P, PACK, S], F32)
-        s5 = tile("s5", [P, PACK, S], F32)
+        s5 = [tile("s5_%d" % u, [P, PACK, W], F32) for u in range(2)]
         for t in range(PACK):
             nc.scalar.activation(out=s4[:, t, :], in_=s_win[t][:].indirect(n4_l[:]), func=ACT.Copy, scale=0.0625)
-            nc.scalar.activation(out=s5[:, t, :], in_=s_win[t][:].indirect(n5_l[:]), func=ACT.Copy, scale=0.75 * 0.0625)
+        for u in range(2):
+            for t in range(PACK):
+                nc.scalar.activation(
+                    out=s5[u][:, t, :], in_=s_win[t][:].indirect(n5_l[:, 8 * u : 8 * (u + 1)]),
+                    func=ACT.Copy, scale=0.75 * 0.0625,
+                )
 
-        w3_c = deal(nc.scalar.copy, "w3_c", w3_raw, U32, "s_win3")
-        za = tile("za", [P, PACK, S], F32)
-        zb = tile("zb", [P, PACK, S], F32)
+        za = tile("za", [P, PACK, S], F32, "key_words")
         for t in range(PACK):
             nc.vector.tensor_tensor(
                 out=za[:, t, :], in0=y_win[t][:].indirect(n2_l[:]), in1=sig3[:, t, :], op=ALU.mult
             )
-        for t in range(PACK):
-            nc.vector.tensor_tensor(out=zb[:, t, :], in0=y1[:, t, :], in1=sig_win[t][:, :S], op=ALU.mult)
-        z_c, z_s = quantise("z", add_and_group("z_grouped", za, zb))
-        w2_c = deal(nc.vector.tensor_copy, "w2_c", w2_raw, U32)
         w23_s = deal(nc.vector.tensor_copy, "w23_s", w23_plane, U8)
-        h_ps = [psum.tile([P, S], F32, name="h_ps%d" % t, tag="yh%d" % t) for t in range(PACK)]
-        for t in range(PACK):
-            mx(h_ps[t][:], w2_c, w23_s, t, z_c, z_s, True, False)
+        w23_c = tile("w23_c", [P, 2, N], U32)
+        nc.vector.tensor_copy(
+            out=w23_c[:].rearrange("p w (t m) -> p w m t", t=PACK),
+            in_=w23_raw[:].rearrange("p w (m t) -> p w m t", t=PACK),
+        )
+        w2_c, w3_c = w23_c[:, 0, :], w23_c[:, 1, :]
+        z_c, z_s = quantise("z", add_and_group("z_grouped", za[:], zb[:], "x_tab"))
+        h_ps = [
+            [psum.tile([P, W], F32, name="h_ps%d_%d" % (u, t), tag="%sh%d" % ("ys"[u], t)) for t in range(PACK)]
+            for u in range(2)
+        ]
+        for u in range(2):
+            cols = slice(W * u, W * (u + 1))
+            for t in range(PACK):
+                mx(h_ps[u][t][:], w2_c, w23_s, t, z_c[:, cols], z_s[:, cols], True, False)
 
-        z2_c, z2_s = quantise("z2", add_and_group("z2_grouped", s4, s5))
-        for t in range(PACK):
-            mx(h_ps[t][:], w3_c, w23_s[4:P, :], t, z2_c, z2_s, False, True)
+        h_win = [tile("h_win%d" % t, [P, S], F32) for t in range(PACK)]
+        for u in range(2):
+            cols = slice(W * u, W * (u + 1))
+            z2_c, z2_s = quantise("z2_%d" % u, add_and_group("z2_grouped%d" % u, s4[:, :, cols], s5[u][:], "x_tab"))
+            for t in range(PACK):
+                mx(h_ps[u][t][:], w3_c, w23_s[4:P, :], t, z2_c[:], z2_s[:], False, True)
+        for u in range(2):
+            for t in range(PACK):
+                nc.vector.tensor_copy(out=h_win[t][:, W * u : W * (u + 1)], in_=h_ps[u][t][:])
 
         out_rows = out_0.rearrange("(p t) s -> p t s", t=PACK)
         out_grouped = tile("out_grouped", [P, S, PACK], BF16)
-        h_win = [tile("h_win%d" % t, [P, S], F32) for t in range(PACK)]
         gate = [tile("gate%d" % t, [P, W], F32) for t in range(PACK)]
         ra = [tile("ra%d" % t, [P, W], F32) for t in range(PACK)]
-        for t in range(PACK):
-            nc.vector.tensor_copy(out=h_win[t][:], in_=h_ps[t][:])
         for t in range(PACK):
             nc.scalar.activation(out=gate[t][:], in_=h_win[t][:].indirect(n7_l[:]), func=ACT.Sigmoid)
             nc.vector.tensor_tensor(

@@ -14,7 +14,10 @@ ACT = mybir.ActivationFunctionType
 
 P = 128
 PACK = 4
-K, T, S, N, H, G, W = 512, 1024, 256, 512, 512, 2048, 128
+QUADS = 4
+LINE = 4
+K, S, N, H, G = 512, 256, 512, 512, 2048
+W = S // 2
 ONE_LIST_WINDOW = S + 16
 EIGHT_LIST_WINDOW = 2 * S
 
@@ -31,51 +34,48 @@ def tile_picked_jkeywsumsumfold_none_po_kernel(
         sb = ctx.enter_context(tc.tile_pool(name="sb", bufs=1))
         psum = ctx.enter_context(tc.psum_pool(name="psum", bufs=1))
 
-        def tile(name, shape, dtype, tag=None):
-            return sb.tile(shape, dtype, name=name, tag=tag or name, align_bytes=64)
+        def tile(name, shape, dtype, reuses=None):
+            return sb.tile(shape, dtype, name=name, tag=reuses or name, align_bytes=64)
+
+        def words_in_hbm(src):
+            return src[0].rearrange("p n t -> p (n t)").bitcast(I32)
+
+        def rows_in_hbm(src, q):
+            return src[0, 4 * q : 4 * q + 4, :].bitcast(I32)
 
         def load_list(name, src):
             lst = tile(name, list(src.shape), U16)
             nc.sync.dma_start(lst[:], src)
             return lst
 
-        def load_words(name, src, tag=None):
-            words = tile(name, [P, src.shape[2]], U32, tag)
-            nc.sync.dma_start(words[:].bitcast(I32), src[0].rearrange("p n t -> p (n t)").bitcast(I32))
+        def load_words(name, src):
+            words = tile(name, [P, src.shape[2]], U32)
+            nc.sync.dma_start(words[:].bitcast(I32), words_in_hbm(src))
             return words
 
-        def zeroed_bytes(name, width, engine, tag=None):
-            plane = tile(name, [P, width], U8, tag)
-            engine.memset(plane[:].bitcast(I32), 0)
-            return plane
+        def load_gains(name, src):
+            gains = tile(name, [P, PACK], F32)
+            nc.sync.dma_start(gains[:], src.rearrange("(p t) o -> p (t o)", t=PACK))
+            return gains
 
-        def load_scale_plane(name, src, quadrants, plane=None):
-            width = src.shape[2]
-            plane = tile(name, [P, width], U8) if plane is None else plane
-            for q in quadrants:
-                rows = src[0, 4 * q : 4 * q + 4, :].bitcast(I32)
-                nc.sync.dma_start(
-                    plane[32 * q : 32 * q + 32, :].bitcast(I32),
-                    rows.unsqueeze(0).to_broadcast([8, 4, width // 4]),
-                )
+        def zeroed_bytes(name, width, engine, reuses=None):
+            plane = tile(name, [P, width], U8, reuses)
+            engine.memset(plane[:].bitcast(I32), 0)
             return plane
 
         def load_scale_rows(plane, src, first, quadrants):
             for q in quadrants:
-                nc.sync.dma_start(
-                    plane[32 * q + first : 32 * q + first + 4, :].bitcast(I32),
-                    src[0, 4 * q : 4 * q + 4, :].bitcast(I32),
-                )
+                nc.sync.dma_start(plane[32 * q + first : 32 * q + first + 4, :].bitcast(I32), rows_in_hbm(src, q))
 
-        def deal(copy, name, src, dtype, tag=None):
-            dealt = tile(name, [P, src.shape[1]], dtype, tag)
-            copy(
+        def deal(name, src, dtype, reuses=None):
+            dealt = tile(name, [P, src.shape[1]], dtype, reuses)
+            nc.vector.tensor_copy(
                 out=dealt[:].rearrange("p (t m) -> p m t", t=PACK),
                 in_=src[:].rearrange("p (m t) -> p m t", t=PACK),
             )
             return dealt
 
-        def gather(name, window, lst, dtype):
+        def gather_packed(name, window, lst, dtype):
             picked = tile(name, [P, lst.shape[1] * 16], dtype)
             nc.vector.tensor_copy(out=picked[:], in_=window[:].indirect(lst[:]))
             return picked
@@ -94,54 +94,57 @@ def tile_picked_jkeywsumsumfold_none_po_kernel(
             nc.vector.quantize_mx(out=codes[:].bitcast(FP8X4), scales=scales[:], in_=grouped[:])
             return codes, scales
 
-        def add_and_group(name, a, b, tag=None):
-            grouped = tile(name, [P, a.shape[2] * PACK], BF16, tag)
+        def add_and_group(name, a, b, reuses):
+            grouped = tile(name, [P, a.shape[2] * PACK], BF16, reuses)
             nc.vector.tensor_tensor(
-                out=grouped[:].rearrange("p (c i t) -> p c t i", i=4, t=PACK),
-                in0=a.rearrange("p t (c i) -> p c t i", i=4),
-                in1=b.rearrange("p t (c i) -> p c t i", i=4),
+                out=grouped[:].rearrange("p (c i t) -> p c t i", i=LINE, t=PACK),
+                in0=a.rearrange("p t (c i) -> p c t i", i=LINE),
+                in1=b.rearrange("p t (c i) -> p c t i", i=LINE),
                 op=ALU.add,
             )
             return grouped
 
-        def windows(name, width, engine):
+        def windows(name, width):
             tiles = [tile("%s%d" % (name, t), [P, width], F32) for t in range(PACK)]
             for win in tiles:
-                engine.memset(win[:, S:], 0.0)
+                nc.vector.memset(win[:, S:], 0.0)
             return tiles
 
         w1_plane = zeroed_bytes("w1_plane", H, nc.vector)
         d_rows = zeroed_bytes("d_rows", G, nc.gpsimd)
         key_plane = zeroed_bytes("key_plane", H, nc.vector)
-        sig_win = windows("sig_win", ONE_LIST_WINDOW, nc.vector)
-        y_win = windows("y_win", ONE_LIST_WINDOW, nc.vector)
-        s_win = windows("s_win", EIGHT_LIST_WINDOW, nc.vector)
+        sig_win = windows("sig_win", ONE_LIST_WINDOW)
+        y_win = windows("y_win", ONE_LIST_WINDOW)
+        s_win = windows("s_win", EIGHT_LIST_WINDOW)
 
         offs_l = load_list("offs_l", offs)
-        x_plane = load_scale_plane("x_plane", x_scales, range(4))
+        x_plane = tile("x_plane", [P, x_scales.shape[2]], U8)
+        for q in range(QUADS):
+            nc.sync.dma_start(
+                x_plane[32 * q : 32 * q + 32, :].bitcast(I32),
+                rows_in_hbm(x_scales, q).unsqueeze(0).to_broadcast([8, 4, x_scales.shape[2] // 4]),
+            )
         load_scale_rows(w1_plane, w1_scales, 0, range(1))
         x_tab = load_words("x_tab", x_words)
         w1_raw = load_words("w1_raw", w1_words)
-        load_scale_rows(w1_plane, w1_scales, 0, range(1, 4))
+        load_scale_rows(w1_plane, w1_scales, 0, range(1, QUADS))
         kidx_l = load_list("kidx_l", kidx)
         nc.sync.dma_start(d_rows[0:P:8, :].bitcast(I32), d_scales[0].bitcast(I32))
-        gn_t = tile("gn_t", [P, PACK], F32)
-        nc.sync.dma_start(gn_t[:], gn.rearrange("(p t) o -> p (t o)", t=PACK))
+        gn_t = load_gains("gn_t", gn)
         n1_l = load_list("n1_l", n1)
         two_l = load_list("two_l", two)
         d_tab = load_words("d_tab", d_words)
         n3_l = load_list("n3_l", n3)
-        gk_t = tile("gk_t", [P, PACK], F32)
-        nc.sync.dma_start(gk_t[:], gk.rearrange("(p t) o -> p (t o)", t=PACK))
+        gk_t = load_gains("gk_t", gk)
         n4_l = load_list("n4_l", n4)
         n5_l = load_list("n5_l", n5)
         n2_l = load_list("n2_l", n2)
         n7_l = load_list("n7_l", n7)
         n6_l = load_list("n6_l", n6)
 
-        xq_s = gather("xq_s", x_plane, offs_l, U8)
-        xq_c = gather("xq_c", x_tab, offs_l, U32)
-        w1_c = deal(nc.vector.tensor_copy, "w1_c", w1_raw, U32)
+        xq_s = gather_packed("xq_s", x_plane, offs_l, U8)
+        xq_c = gather_packed("xq_c", x_tab, offs_l, U32)
+        w1_c = deal("w1_c", w1_raw, U32)
         w1_s = tile("w1_s", [P, H], U8)
         for t in range(PACK):
             nc.vector.tensor_copy(out=w1_s[:, P * t : P * (t + 1)], in_=w1_plane[:, t:H:PACK])
@@ -151,13 +154,14 @@ def tile_picked_jkeywsumsumfold_none_po_kernel(
         for t in range(PACK):
             nc.scalar.activation(out=sig_win[t][:, :S], in_=y_ps[t][:], func=ACT.Sigmoid)
 
-        key_rows = gather("key_rows", d_rows, kidx_l, U8)
-        key_dealt = deal(nc.vector.tensor_copy, "key_dealt", key_rows, U8)
-        for q in range(4):
+        key_rows = gather_packed("key_rows", d_rows, kidx_l, U8)
+        key_dealt = deal("key_dealt", key_rows, U8)
+        for q in range(QUADS):
             nc.sync.dma_start(
                 key_plane[32 * q : 32 * q + 4, :].bitcast(I32),
                 key_dealt[32 * q : 32 * q + 32 : 8, :].bitcast(I32),
             )
+
         sig3 = tile("sig3", [P, PACK, S], F32)
         y1 = tile("y1", [P, PACK, S], F32)
         for t in range(PACK):
@@ -170,31 +174,36 @@ def tile_picked_jkeywsumsumfold_none_po_kernel(
             nc.gpsimd.tensor_tensor(out=zb[:, t, :], in0=y1[:, t, :], in1=sig_win[t][:, :S], op=ALU.mult)
         for t in range(PACK):
             nc.scalar.activation(out=sig3[:, t, :], in_=sig_win[t][:].indirect(n3_l[:]), func=ACT.Copy)
-        xt_s = gather("xt_s", x_plane, two_l, U8)
-        xt_c = gather("xt_c", x_tab, two_l, U32)
-        w23_plane = zeroed_bytes("w23_plane", N, nc.vector, "x_plane")
-        load_scale_rows(w23_plane, w2_scales, 0, range(4))
-        load_scale_rows(w23_plane, w3_scales, 4, range(4))
+
+        xt_s = gather_packed("xt_s", x_plane, two_l, U8)
+        xt_c = gather_packed("xt_c", x_tab, two_l, U32)
+        w23_plane = zeroed_bytes("w23_plane", N, nc.gpsimd, "x_plane")
+        load_scale_rows(w23_plane, w2_scales, 0, range(QUADS))
+        load_scale_rows(w23_plane, w3_scales, 4, range(QUADS))
         w23_raw = tile("w23_raw", [P, 2, N], U32, "x_tab")
         for i, src in enumerate((w2_words, w3_words)):
-            nc.sync.dma_start(w23_raw[:, i, :].bitcast(I32), src[0].rearrange("p n t -> p (n t)").bitcast(I32))
+            nc.sync.dma_start(w23_raw[:, i, :].bitcast(I32), words_in_hbm(src))
 
-        key_words = gather("key_words", d_tab, kidx_l, U32)
-        key_c = deal(nc.vector.tensor_copy, "key_c", key_words, U32)
+        key_words = gather_packed("key_words", d_tab, kidx_l, U32)
+        key_c = deal("key_c", key_words, U32)
         s_ps = [psum.tile([P, S], F32, name="s_ps%d" % t, tag="sh%d" % t) for t in range(PACK)]
         for t in range(PACK):
             mx(s_ps[t][:], key_c, key_plane, t, xt_c[:], xt_s[:], True, True)
-        for t in range(PACK):
+        for t in range(PACK - 1):
             nc.scalar.activation(out=s_win[t][:, :S], in_=s_ps[t][:], func=ACT.Copy, scale=gk_t[:, t : t + 1])
+        nc.vector.tensor_scalar(
+            out=s_win[-1][:, :S], in0=s_ps[-1][:], scalar1=gk_t[:, PACK - 1 : PACK], scalar2=None, op0=ALU.mult
+        )
+        halves = [slice(W * u, W * (u + 1)) for u in range(2)]
         s4 = tile("s4", [P, PACK, S], F32)
         s5 = [tile("s5_%d" % u, [P, PACK, W], F32) for u in range(2)]
         for t in range(PACK):
             nc.scalar.activation(out=s4[:, t, :], in_=s_win[t][:].indirect(n4_l[:]), func=ACT.Copy, scale=0.0625)
         for u in range(2):
+            entries = n5_l[:, W // 16 * u : W // 16 * (u + 1)]
             for t in range(PACK):
                 nc.scalar.activation(
-                    out=s5[u][:, t, :], in_=s_win[t][:].indirect(n5_l[:, 8 * u : 8 * (u + 1)]),
-                    func=ACT.Copy, scale=0.75 * 0.0625,
+                    out=s5[u][:, t, :], in_=s_win[t][:].indirect(entries), func=ACT.Copy, scale=0.75 * 0.0625
                 )
 
         za = tile("za", [P, PACK, S], F32, "key_words")
@@ -202,35 +211,36 @@ def tile_picked_jkeywsumsumfold_none_po_kernel(
             nc.vector.tensor_tensor(
                 out=za[:, t, :], in0=y_win[t][:].indirect(n2_l[:]), in1=sig3[:, t, :], op=ALU.mult
             )
-        w23_s = deal(nc.vector.tensor_copy, "w23_s", w23_plane, U8)
         w23_c = tile("w23_c", [P, 2, N], U32)
         nc.vector.tensor_copy(
             out=w23_c[:].rearrange("p w (t m) -> p w m t", t=PACK),
             in_=w23_raw[:].rearrange("p w (m t) -> p w m t", t=PACK),
         )
         w2_c, w3_c = w23_c[:, 0, :], w23_c[:, 1, :]
-        z_c, z_s = quantise("z", add_and_group("z_grouped", za[:], zb[:], "x_tab"))
+        z_grouped = add_and_group("z_grouped", za[:], zb[:], "x_tab")
+        w23_s = deal("w23_s", w23_plane, U8, "zb")
+        z_c, z_s = quantise("z", z_grouped)
         h_ps = [
             [psum.tile([P, W], F32, name="h_ps%d_%d" % (u, t), tag="%sh%d" % ("ys"[u], t)) for t in range(PACK)]
             for u in range(2)
         ]
         for u in range(2):
-            cols = slice(W * u, W * (u + 1))
             for t in range(PACK):
-                mx(h_ps[u][t][:], w2_c, w23_s, t, z_c[:, cols], z_s[:, cols], True, False)
+                mx(h_ps[u][t][:], w2_c, w23_s, t, z_c[:, halves[u]], z_s[:, halves[u]], True, False)
 
         h_win = [tile("h_win%d" % t, [P, S], F32) for t in range(PACK)]
         for u in range(2):
-            cols = slice(W * u, W * (u + 1))
-            z2_c, z2_s = quantise("z2_%d" % u, add_and_group("z2_grouped%d" % u, s4[:, :, cols], s5[u][:], "x_tab"))
+            z2_grouped = add_and_group("z2_grouped%d" % u, s4[:, :, halves[u]], s5[u][:], "x_tab")
+            z2_c, z2_s = quantise("z2_%d" % u, z2_grouped)
             for t in range(PACK):
                 mx(h_ps[u][t][:], w3_c, w23_s[4:P, :], t, z2_c[:], z2_s[:], False, True)
-        for u in range(2):
-            for t in range(PACK):
-                nc.vector.tensor_copy(out=h_win[t][:, W * u : W * (u + 1)], in_=h_ps[u][t][:])
+        for t in range(PACK):
+            nc.scalar.copy(out=h_win[t][:, halves[0]], in_=h_ps[0][t][:])
+        for t in range(PACK):
+            nc.vector.tensor_copy(out=h_win[t][:, halves[1]], in_=h_ps[1][t][:])
 
         out_rows = out_0.rearrange("(p t) s -> p t s", t=PACK)
-        out_grouped = tile("out_grouped", [P, S, PACK], BF16)
+        out_grouped = [tile("out_grouped%d" % u, [P, W, PACK], BF16) for u in range(2)]
         gate = [tile("gate%d" % t, [P, W], F32) for t in range(PACK)]
         ra = [tile("ra%d" % t, [P, W], F32) for t in range(PACK)]
         for t in range(PACK):
@@ -241,16 +251,17 @@ def tile_picked_jkeywsumsumfold_none_po_kernel(
         for t in range(PACK):
             nc.scalar.activation(out=h_win[t][:].indirect(n7_l[:]), in_=ra[t][:], func=ACT.Copy)
             nc.sync.dma_start(out_rows[:, t, :], h_win[t][:])
-            nc.vector.tensor_copy(out=out_grouped[:, :, t], in_=h_win[t][:])
+            for u in range(2):
+                nc.vector.tensor_copy(out=out_grouped[u][:, :, t], in_=h_win[t][:, halves[u]])
 
         out_c = tile("out_c", [P, S], U32)
         out_s = tile("out_s", [P, S], U8)
-        nc.vector.quantize_mx(
-            out=out_c[:].bitcast(FP8X4), scales=out_s[:], in_=out_grouped[:].rearrange("p s t -> p (s t)")
-        )
-        nc.sync.dma_start(out_1[0].rearrange("p n t -> p (n t)").bitcast(I32), out_c[:].bitcast(I32))
-        for q in range(4):
-            eng = nc.scalar if q % 2 else nc.sync
-            eng.dma_start(
-                out_2[0, 4 * q : 4 * q + 4, :].bitcast(I32), out_s[32 * q : 32 * q + 4, :].bitcast(I32)
+        for u in range(2):
+            nc.vector.quantize_mx(
+                out=out_c[:, halves[u]].bitcast(FP8X4), scales=out_s[:, halves[u]],
+                in_=out_grouped[u][:].rearrange("p s t -> p (s t)"),
             )
+        nc.sync.dma_start(words_in_hbm(out_1), out_c[:].bitcast(I32))
+        for q in range(QUADS):
+            queue = nc.scalar if q % 2 else nc.sync
+            queue.dma_start(rows_in_hbm(out_2, q), out_s[32 * q : 32 * q + 4, :].bitcast(I32))

from contextlib import ExitStack

import concourse.mybir as mybir

F32 = mybir.dt.float32
BF16 = mybir.dt.bfloat16
I32 = mybir.dt.int32
U32 = mybir.dt.uint32
U16 = mybir.dt.uint16
U8 = mybir.dt.uint8
FP8X4 = mybir.dt.float8_e4m3fn_x4
ALU = mybir.AluOpType
ACT = mybir.ActivationFunctionType

P = 128
PACK = 4
QUADS = 4
LINE = 4
K, S, N, H, G = 512, 256, 512, 512, 2048
W = S // 2
ONE_LIST_WINDOW = S + 16
EIGHT_LIST_WINDOW = 2 * S

FLOPS = 4 * 2 * K * H * S


def tile_picked_jkeywsumsumfold_none_po_kernel(
    tc, x_words, x_scales, w1_words, w1_scales, d_words, d_scales, gn, gk,
    w2_words, w2_scales, w3_words, w3_scales,
    offs, kidx, two, n1, n2, n3, n4, n5, n6, n7, out_0, out_1, out_2,
):
    nc = tc.nc
    with ExitStack() as ctx:
        sb = ctx.enter_context(tc.tile_pool(name="sb", bufs=1))
        psum = ctx.enter_context(tc.psum_pool(name="psum", bufs=1))

        def tile(name, shape, dtype, reuses=None):
            return sb.tile(shape, dtype, name=name, tag=reuses or name, align_bytes=64)

        def words_in_hbm(src):
            return src[0].rearrange("p n t -> p (n t)").bitcast(I32)

        def rows_in_hbm(src, q):
            return src[0, 4 * q : 4 * q + 4, :].bitcast(I32)

        def load_list(name, src):
            lst = tile(name, list(src.shape), U16)
            nc.sync.dma_start(lst[:], src)
            return lst

        def load_words(name, src):
            words = tile(name, [P, src.shape[2]], U32)
            nc.sync.dma_start(words[:].bitcast(I32), words_in_hbm(src))
            return words

        def load_gains(name, src):
            gains = tile(name, [P, PACK], F32)
            nc.sync.dma_start(gains[:], src.rearrange("(p t) o -> p (t o)", t=PACK))
            return gains

        def zeroed_bytes(name, width, engine, reuses=None):
            plane = tile(name, [P, width], U8, reuses)
            engine.memset(plane[:].bitcast(I32), 0)
            return plane

        def load_scale_rows(plane, src, first, quadrants):
            for q in quadrants:
                nc.sync.dma_start(plane[32 * q + first : 32 * q + first + 4, :].bitcast(I32), rows_in_hbm(src, q))

        def deal(name, src, dtype, reuses=None):
            dealt = tile(name, [P, src.shape[1]], dtype, reuses)
            nc.vector.tensor_copy(
                out=dealt[:].rearrange("p (t m) -> p m t", t=PACK),
                in_=src[:].rearrange("p (m t) -> p m t", t=PACK),
            )
            return dealt

        def gather_packed(name, window, lst, dtype):
            picked = tile(name, [P, lst.shape[1] * 16], dtype)
            nc.vector.tensor_copy(out=picked[:], in_=window[:].indirect(lst[:]))
            return picked

        def mx(out, words, scales, t, rhs, rhs_scales, start, stop):
            cols = slice(P * t, P * (t + 1))
            nc.tensor.matmul_mx(
                out=out, lhsT=words[:, cols].bitcast(FP8X4), lhsT_scale=scales[:, cols],
                rhs=rhs.bitcast(FP8X4), rhs_scale=rhs_scales, start=start, stop=stop,
            )

        def quantise(name, grouped):
            width = grouped.shape[1] // PACK
            codes = tile(name + "_codes", [P, width], U32)
            scales = tile(name + "_scales", [P, width], U8)
            nc.vector.quantize_mx(out=codes[:].bitcast(FP8X4), scales=scales[:], in_=grouped[:])
            return codes, scales

        def add_and_group(name, a, b, reuses):
            grouped = tile(name, [P, a.shape[2] * PACK], BF16, reuses)
            nc.vector.tensor_tensor(
                out=grouped[:].rearrange("p (c i t) -> p c t i", i=LINE, t=PACK),
                in0=a.rearrange("p t (c i) -> p c t i", i=LINE),
                in1=b.rearrange("p t (c i) -> p c t i", i=LINE),
                op=ALU.add,
            )
            return grouped

        def windows(name, width):
            tiles = [tile("%s%d" % (name, t), [P, width], F32) for t in range(PACK)]
            for win in tiles:
                nc.vector.memset(win[:, S:], 0.0)
            return tiles

        w1_plane = zeroed_bytes("w1_plane", H, nc.vector)
        d_rows = zeroed_bytes("d_rows", G, nc.gpsimd)
        key_plane = zeroed_bytes("key_plane", H, nc.vector)
        sig_win = windows("sig_win", ONE_LIST_WINDOW)
        y_win = windows("y_win", ONE_LIST_WINDOW)
        s_win = windows("s_win", EIGHT_LIST_WINDOW)

        offs_l = load_list("offs_l", offs)
        x_plane = tile("x_plane", [P, x_scales.shape[2]], U8)
        for q in range(QUADS):
            nc.sync.dma_start(
                x_plane[32 * q : 32 * q + 32, :].bitcast(I32),
                rows_in_hbm(x_scales, q).unsqueeze(0).to_broadcast([8, 4, x_scales.shape[2] // 4]),
            )
        load_scale_rows(w1_plane, w1_scales, 0, range(1))
        x_tab = load_words("x_tab", x_words)
        w1_raw = load_words("w1_raw", w1_words)
        load_scale_rows(w1_plane, w1_scales, 0, range(1, QUADS))
        kidx_l = load_list("kidx_l", kidx)
        nc.sync.dma_start(d_rows[0:P:8, :].bitcast(I32), d_scales[0].bitcast(I32))
        gn_t = load_gains("gn_t", gn)
        n1_l = load_list("n1_l", n1)
        two_l = load_list("two_l", two)
        d_tab = load_words("d_tab", d_words)
        n3_l = load_list("n3_l", n3)
        gk_t = load_gains("gk_t", gk)
        n4_l = load_list("n4_l", n4)
        n5_l = load_list("n5_l", n5)
        n2_l = load_list("n2_l", n2)
        n7_l = load_list("n7_l", n7)
        n6_l = load_list("n6_l", n6)

        xq_s = gather_packed("xq_s", x_plane, offs_l, U8)
        xq_c = gather_packed("xq_c", x_tab, offs_l, U32)
        w1_c = deal("w1_c", w1_raw, U32)
        w1_s = tile("w1_s", [P, H], U8)
        for t in range(PACK):
            nc.vector.tensor_copy(out=w1_s[:, P * t : P * (t + 1)], in_=w1_plane[:, t:H:PACK])
        y_ps = [psum.tile([P, S], F32, name="y_ps%d" % t, tag="yh%d" % t) for t in range(PACK)]
        for t in range(PACK):
            mx(y_ps[t][:], w1_c, w1_s, t, xq_c[:], xq_s[:], True, True)
        for t in range(PACK):
            nc.scalar.activation(out=sig_win[t][:, :S], in_=y_ps[t][:], func=ACT.Sigmoid)

        key_rows = gather_packed("key_rows", d_rows, kidx_l, U8)
        key_dealt = deal("key_dealt", key_rows, U8)
        for q in range(QUADS):
            nc.sync.dma_start(
                key_plane[32 * q : 32 * q + 4, :].bitcast(I32),
                key_dealt[32 * q : 32 * q + 32 : 8, :].bitcast(I32),
            )

        sig3 = tile("sig3", [P, PACK, S], F32)
        y1 = tile("y1", [P, PACK, S], F32)
        for t in range(PACK):
            nc.vector.tensor_scalar(
                out=y_win[t][:, :S], in0=y_ps[t][:], scalar1=gn_t[:, t : t + 1], scalar2=None, op0=ALU.mult
            )
        zb = tile("zb", [P, PACK, S], F32)
        for t in range(PACK):
            nc.scalar.activation(out=y1[:, t, :], in_=y_win[t][:].indirect(n1_l[:]), func=ACT.Copy)
            nc.gpsimd.tensor_tensor(out=zb[:, t, :], in0=y1[:, t, :], in1=sig_win[t][:, :S], op=ALU.mult)
        for t in range(PACK):
            nc.scalar.activation(out=sig3[:, t, :], in_=sig_win[t][:].indirect(n3_l[:]), func=ACT.Copy)

        xt_s = gather_packed("xt_s", x_plane, two_l, U8)
        xt_c = gather_packed("xt_c", x_tab, two_l, U32)
        w23_plane = zeroed_bytes("w23_plane", N, nc.gpsimd, "x_plane")
        load_scale_rows(w23_plane, w2_scales, 0, range(QUADS))
        load_scale_rows(w23_plane, w3_scales, 4, range(QUADS))
        w23_raw = tile("w23_raw", [P, 2, N], U32, "x_tab")
        for i, src in enumerate((w2_words, w3_words)):
            nc.sync.dma_start(w23_raw[:, i, :].bitcast(I32), words_in_hbm(src))

        key_words = gather_packed("key_words", d_tab, kidx_l, U32)
        key_c = deal("key_c", key_words, U32)
        s_ps = [psum.tile([P, S], F32, name="s_ps%d" % t, tag="sh%d" % t) for t in range(PACK)]
        for t in range(PACK):
            mx(s_ps[t][:], key_c, key_plane, t, xt_c[:], xt_s[:], True, True)
        for t in range(PACK - 1):
            nc.scalar.activation(out=s_win[t][:, :S], in_=s_ps[t][:], func=ACT.Copy, scale=gk_t[:, t : t + 1])
        nc.vector.tensor_scalar(
            out=s_win[-1][:, :S], in0=s_ps[-1][:], scalar1=gk_t[:, PACK - 1 : PACK], scalar2=None, op0=ALU.mult
        )
        halves = [slice(W * u, W * (u + 1)) for u in range(2)]
        s4 = tile("s4", [P, PACK, S], F32)
        s5 = [tile("s5_%d" % u, [P, PACK, W], F32) for u in range(2)]
        for t in range(PACK):
            nc.scalar.activation(out=s4[:, t, :], in_=s_win[t][:].indirect(n4_l[:]), func=ACT.Copy, scale=0.0625)
        for u in range(2):
            entries = n5_l[:, W // 16 * u : W // 16 * (u + 1)]
            for t in range(PACK):
                nc.scalar.activation(
                    out=s5[u][:, t, :], in_=s_win[t][:].indirect(entries), func=ACT.Copy, scale=0.75 * 0.0625
                )

        za = tile("za", [P, PACK, S], F32, "key_words")
        for t in range(PACK):
            nc.vector.tensor_tensor(
                out=za[:, t, :], in0=y_win[t][:].indirect(n2_l[:]), in1=sig3[:, t, :], op=ALU.mult
            )
        w23_c = tile("w23_c", [P, 2, N], U32)
        nc.vector.tensor_copy(
            out=w23_c[:].rearrange("p w (t m) -> p w m t", t=PACK),
            in_=w23_raw[:].rearrange("p w (m t) -> p w m t", t=PACK),
        )
        w2_c, w3_c = w23_c[:, 0, :], w23_c[:, 1, :]
        z_grouped = add_and_group("z_grouped", za[:], zb[:], "x_tab")
        w23_s = deal("w23_s", w23_plane, U8, "zb")
        z_c, z_s = quantise("z", z_grouped)
        h_ps = [
            [psum.tile([P, W], F32, name="h_ps%d_%d" % (u, t), tag="%sh%d" % ("ys"[u], t)) for t in range(PACK)]
            for u in range(2)
        ]
        for u in range(2):
            for t in range(PACK):
                mx(h_ps[u][t][:], w2_c, w23_s, t, z_c[:, halves[u]], z_s[:, halves[u]], True, False)

        h_win = [tile("h_win%d" % t, [P, S], F32) for t in range(PACK)]
        for u in range(2):
            z2_grouped = add_and_group("z2_grouped%d" % u, s4[:, :, halves[u]], s5[u][:], "x_tab")
            z2_c, z2_s = quantise("z2_%d" % u, z2_grouped)
            for t in range(PACK):
                mx(h_ps[u][t][:], w3_c, w23_s[4:P, :], t, z2_c[:], z2_s[:], False, True)
        for t in range(PACK):
            nc.scalar.copy(out=h_win[t][:, halves[0]], in_=h_ps[0][t][:])
        for t in range(PACK):
            nc.vector.tensor_copy(out=h_win[t][:, halves[1]], in_=h_ps[1][t][:])

        out_rows = out_0.rearrange("(p t) s -> p t s", t=PACK)
        out_grouped = [tile("out_grouped%d" % u, [P, W, PACK], BF16) for u in range(2)]
        gate = [tile("gate%d" % t, [P, W], F32) for t in range(PACK)]
        ra = [tile("ra%d" % t, [P, W], F32) for t in range(PACK)]
        for t in range(PACK):
            nc.scalar.activation(out=gate[t][:], in_=h_win[t][:].indirect(n7_l[:]), func=ACT.Sigmoid)
            nc.vector.tensor_tensor(
                out=ra[t][:], in0=h_win[t][:].indirect(n6_l[:]), in1=gate[t][:], op=ALU.mult
            )
        for t in range(PACK):
            nc.scalar.activation(out=h_win[t][:].indirect(n7_l[:]), in_=ra[t][:], func=ACT.Copy)
            nc.sync.dma_start(out_rows[:, t, :], h_win[t][:])
            for u in range(2):
                nc.vector.tensor_copy(out=out_grouped[u][:, :, t], in_=h_win[t][:, halves[u]])

        out_c = tile("out_c", [P, S], U32)
        out_s = tile("out_s", [P, S], U8)
        for u in range(2):
            nc.vector.quantize_mx(
                out=out_c[:, halves[u]].bitcast(FP8X4), scales=out_s[:, halves[u]],
                in_=out_grouped[u][:].rearrange("p s t -> p (s t)"),
            )
        nc.sync.dma_start(words_in_hbm(out_1), out_c[:].bitcast(I32))
        for q in range(QUADS):
            queue = nc.scalar if q % 2 else nc.sync
            queue.dma_start(rows_in_hbm(out_2, q), out_s[32 * q : 32 * q + 4, :].bitcast(I32))
